import numpy as np
import ml_dtypes


def mxq(x, axis, fmt="e4m3"):
    dtype, down = {"e4m3": (ml_dtypes.float8_e4m3fn, 7), "e5m2": (ml_dtypes.float8_e5m2, 14)}[fmt]
    v = np.moveaxis(np.asarray(x, np.float32).astype(ml_dtypes.bfloat16).astype(np.float64), axis, -1)
    blocks = v.reshape(v.shape[:-1] + (-1, 32))
    amax = np.abs(blocks).max(-1, keepdims=True)
    byte = np.maximum(np.where(amax > 0, np.frexp(amax)[1] - 1 + 127, 0) - down, 1)
    scale = np.exp2(byte - 127.0)
    codes = (blocks / scale).astype(np.float32).astype(dtype).astype(np.float64)
    return np.moveaxis((codes * scale).reshape(v.shape), -1, axis)


WIDE = False


def mx_kscale(k):
    if not WIDE:
        return np.ones(k)
    levels = np.array([10, -10, 5, -5, 0])
    if k % 512:
        return np.exp2(np.random.permutation(np.resize(levels, k // 32))).repeat(32)
    a = np.empty((k // 512, 16))
    for p in range(k // 512):
        a[p, :8] = np.random.permutation(np.resize(levels, 8))
        for g in range(8):
            far = levels[np.abs(levels - a[p, g]) >= 10]
            a[p, g + 8] = far[np.random.randint(len(far))]
    return np.exp2(a.ravel()).repeat(32)


BF16 = ml_dtypes.bfloat16


def bf(x):
    return np.asarray(x, np.float32).astype(BF16)


def f64(x):
    return np.asarray(x).astype(np.float64)


E2M1 = np.array([0.0, 0.5, 1.0, 1.5, 2.0, 3.0, 4.0, 6.0, -0.0, -0.5, -1.0, -1.5, -2.0, -3.0, -4.0, -6.0])


def pack_weight(w, fmt):
    k, n = w.shape
    w = f64(bf(w)).reshape(k // 32, 32, n)
    amax = np.abs(w).max(1)
    if fmt == "e4m3":
        byte = np.frexp(amax)[1] - 1 + 127 - 7
    else:
        mant, ex = np.frexp(amax / 6.0)
        byte = np.where(mant > 0.5, ex, ex - 1) + 127
    byte = np.clip(np.where(amax > 0, byte, 1), 1, 254)
    scaled = (w * np.exp2(127.0 - byte)[:, None, :]).reshape(k, n).astype(np.float32)
    by_word = np.ascontiguousarray(scaled.reshape(k // 512, 128, 4, n).transpose(0, 1, 3, 2))
    if fmt == "e4m3":
        words = by_word.astype(ml_dtypes.float8_e4m3fn).view(np.uint8)
    else:
        c = by_word.astype(ml_dtypes.float4_e2m1fn).view(np.uint8) & 0xF
        words = c[..., 0::2] | (c[..., 1::2] << 4)
    return np.ascontiguousarray(words), np.ascontiguousarray(byte.astype(np.uint8).reshape(k // 512, 16, n))


def unpack_weight(words, scales, fmt):
    g, p, n, _ = words.shape
    if fmt == "e4m3":
        vals = np.ascontiguousarray(words).view(ml_dtypes.float8_e4m3fn).astype(np.float64)
    else:
        nib = np.empty((g, p, n, 4), np.uint8)
        nib[..., 0::2] = words & 0xF
        nib[..., 1::2] = words >> 4
        vals = E2M1[nib]
    vals = vals * np.repeat(np.exp2(scales.astype(np.float64) - 127.0), 8, axis=1)[..., None]
    return vals.transpose(0, 1, 3, 2).reshape(g * 512, n)
def pack4(w):
    words, scales = pack_weight(w, "e2m1")
    return words.reshape(words.shape[0], 128, -1), scales


def unpack4(words, scales):
    return unpack_weight(words.reshape(words.shape[0], 128, -1, 2), scales, "e2m1")


B, N, D, H = 512, 2048, 1024, 512


def setup_inputs():
    s1, s2, s3 = mx_kscale(D), mx_kscale(D), mx_kscale(D)
    c1 = np.random.standard_normal((D, N)) * 0.4 / np.sqrt(D)
    c2 = np.random.standard_normal((D, N)) * 0.4 / np.sqrt(D)
    c3 = np.random.standard_normal((D, N)) * 0.4 / np.sqrt(D)
    c1_words, c1_scales = pack4(c1 / s1[:, None])
    c2_words, c2_scales = pack4(c2 / s2[:, None])
    c3_words, c3_scales = pack4(c3 / s3[:, None])
    return {"r": bf(np.random.standard_normal((B, N))),
            "w1": bf(np.random.uniform(0.5, 1.0, D) * s1),
            "w2": bf(np.random.uniform(0.5, 1.0, D) * s2),
            "w3": bf(np.random.uniform(0.5, 1.0, D) * s3),
            "c1_words": c1_words, "c1_scales": c1_scales,
            "c2_words": c2_words, "c2_scales": c2_scales,
            "c3_words": c3_words, "c3_scales": c3_scales}


def reference(r, w1, w2, w3, c1_words, c1_scales, c2_words, c2_scales, c3_words, c3_scales):
    r0 = f64(r)
    a1 = mxq(r0[:, :D] * f64(w1), 1, "e4m3")
    r1 = r0 + (a1 @ unpack4(c1_words, c1_scales))
    a2 = mxq(r1[:, H:H + D] * f64(w2), 1, "e4m3")
    r2 = r1 + (a2 @ unpack4(c2_words, c2_scales))
    a3 = mxq(r2[:, N - D:] * f64(w3), 1, "e4m3")
    r3 = r2 + (a3 @ unpack4(c3_words, c3_scales))
    return r3

@@ -1,0 +1,279 @@
+from contextlib import ExitStack
+
+import concourse.mybir as mybir
+from concourse.masks import make_identity
+
+B, N, D, H = 512, 2048, 1024, 512
+FLOPS = 3 * 2 * B * D * N
+
+F32 = mybir.dt.float32
+BF16 = mybir.dt.bfloat16
+I32 = mybir.dt.int32
+U32 = mybir.dt.uint32
+U8 = mybir.dt.uint8
+FP8X4 = mybir.dt.float8_e4m3fn_x4
+FP4X4 = mybir.dt.float4_e2m1fn_x4
+ADD = mybir.AluOpType.add
+MULT = mybir.AluOpType.mult
+
+P = 128
+CHUNK = 512
+CHUNKS = N // CHUNK
+PASSES = D // CHUNK
+TILES = B // P
+STAGES = 3
+W_ROW = 16
+
+
+def tile_schwarz_three_sweep_t2_kernel(
+    tc, r, w1, w2, w3, c1_words, c1_scales, c2_words, c2_scales, c3_words, c3_scales, out
+):
+    nc = tc.nc
+    w_dram = (w1, w2, w3)
+    words_dram = (c1_words, c2_words, c3_words)
+    scales_dram = (c1_scales, c2_scales, c3_scales)
+
+    with ExitStack() as ctx:
+        sb = ctx.enter_context(tc.tile_pool(name="sb", bufs=1))
+        psum = ctx.enter_context(tc.psum_pool(name="psum", bufs=1))
+        ctx.enter_context(tc.manual_schedule())
+
+        def sbuf(name, shape, dtype):
+            return sb.tile(shape, dtype, name=name, align_bytes=64)
+
+        def bank(tile, chunk):
+            name = "bank_%d_%d" % (tile % 2, chunk)
+            return psum.tile([P, CHUNK], F32, name=name, tag=name)
+
+        ident = sbuf("ident", [P, P], F32)
+        make_identity(nc, ident[:])
+
+        planes = []
+        for s in range(STAGES):
+            plane = sbuf("plane%d" % s, [P, PASSES, N], U8)
+            nc.vector.memset(plane[:].bitcast(I32), 0)
+            planes.append(plane)
+
+        r_half = {}
+        w_cols = {}
+        c_codes = {}
+
+        def load_r(tile, half):
+            t = sbuf("r_%d_%d" % (tile, half), [P, D], BF16)
+            nc.sync.dma_start(out=t[:], in_=r[tile * P : (tile + 1) * P, half * D : (half + 1) * D])
+            r_half[tile, half] = t
+
+        def load_w(s):
+            t = sbuf("w_cols%d" % s, [P, PASSES, W_ROW], BF16)
+            nc.sync.dma_start(out=t[:, :, 0:4], in_=w_dram[s].rearrange("(g p t) -> p g t", g=PASSES, t=4))
+            w_cols[s] = t
+
+        def load_scales(s):
+            src = scales_dram[s].bitcast(I32).rearrange("g (q r) n -> r q g n", r=4)
+            dst = planes[s][:].bitcast(I32)
+            for row in range(4):
+                nc.sync.dma_start(out=dst[row:P:32, :, :], in_=src[row])
+
+        def load_codes(s, first, count):
+            t = sbuf("codes_%d_%d" % (s, first), [P, PASSES, count * 2 * CHUNK], U8)
+            src = words_dram[s].bitcast(I32).rearrange("g p n -> p g n")
+            per_chunk = 2 * CHUNK // 4
+            nc.sync.dma_start(
+                out=t[:].bitcast(I32), in_=src[:, :, first * per_chunk : (first + count) * per_chunk]
+            )
+            for c in range(count):
+                c_codes[s, first + c] = (t, c)
+
+        load_r(0, 0)
+        load_w(0)
+        load_scales(0)
+        load_codes(0, 1, 1)
+        load_codes(0, 2, 1)
+        load_r(0, 1)
+        load_w(1)
+        load_r(1, 0)
+        load_w(2)
+        load_codes(0, 3, 1)
+        load_codes(0, 0, 1)
+        load_r(1, 1)
+        load_scales(1)
+        load_codes(1, 2, 2)
+        load_codes(1, 0, 2)
+        load_r(2, 0)
+        load_scales(2)
+        load_codes(2, 0, 2)
+        load_codes(2, 2, 2)
+        load_r(3, 0)
+        load_r(2, 1)
+        load_r(3, 1)
+
+        base = {}
+        for tile in range(TILES):
+            for c in range(CHUNKS):
+                base[tile, c] = r_half[tile, c // 2][:, (c % 2) * CHUNK : (c % 2 + 1) * CHUNK]
+
+        w_rows = {}
+        sorted_a = {}
+        grouped = {}
+        raw = {}
+        a_codes = {}
+        a_scales = {}
+        groups = {}
+        turned = {}
+
+        def mx(s, tile, chunk, start, stop):
+            if start:
+                groups[tile, chunk] = bank(tile, chunk)
+            acc = groups[tile, chunk]
+            t, c = c_codes[s, chunk]
+            for g in range(PASSES):
+                nc.tensor.matmul_mx(
+                    out=acc[:],
+                    lhsT=a_codes[s, tile][:, g * P : (g + 1) * P].bitcast(FP8X4),
+                    lhsT_scale=a_scales[s, tile][:, g * P : (g + 1) * P],
+                    rhs=t[:, g, c * 2 * CHUNK : (c + 1) * 2 * CHUNK].bitcast(FP4X4),
+                    rhs_scale=planes[s][:, g, chunk * CHUNK : (chunk + 1) * CHUNK],
+                    start=(start and g == 0),
+                    stop=(stop and g == PASSES - 1),
+                )
+
+        def add_base(s, tile, chunk):
+            t = sbuf("res_%d_%d_%d" % (s, tile, chunk), [P, CHUNK], F32)
+            nc.vector.tensor_tensor(out=t[:], in0=groups[tile, chunk][:], in1=base[tile, chunk], op=ADD)
+            base[tile, chunk] = t[:]
+            if s == STAGES - 1:
+                nc.sync.dma_start(
+                    out=out[tile * P : (tile + 1) * P, chunk * CHUNK : (chunk + 1) * CHUNK], in_=t[:]
+                )
+
+        def weigh(s, tile, g):
+            if (s, tile) not in sorted_a:
+                sorted_a[s, tile] = sbuf("sorted_%d_%d" % (s, tile), [P, D], BF16)
+            cols = slice(g * CHUNK, (g + 1) * CHUNK)
+            nc.vector.tensor_tensor(
+                out=sorted_a[s, tile][:, cols].rearrange("p (u m e) -> p u m e", u=2, e=2),
+                in0=base[tile, s + g].rearrange("p (m u e) -> p u m e", u=2, e=2),
+                in1=w_rows[s][:, cols].rearrange("p (u m e) -> p u m e", u=2, e=2),
+                op=MULT,
+            )
+
+        def turn(s, tile, at):
+            t = bank(*at)
+            for g in range(PASSES):
+                for u in range(2):
+                    j = 2 * g + u
+                    if s == 0:
+                        src = r_half[tile, 0][:].bitcast(F32)[:, 2 * P * g + u : 2 * P * (g + 1) : 2]
+                    else:
+                        src = sorted_a[s, tile][:].bitcast(F32)[:, j * P : (j + 1) * P]
+                    nc.tensor.transpose(t[:, j * P : (j + 1) * P], src, ident[:])
+            turned[s, tile] = t
+
+        def spread_w(s, at):
+            t = bank(*at)
+            words = w_cols[s][:].bitcast(F32)
+            for g in range(PASSES):
+                for u in range(2):
+                    j = 2 * g + u
+                    nc.tensor.transpose(
+                        t[:, j * P : (j + 1) * P], words[:, g, u : u + 1].to_broadcast([P, P]), ident[:]
+                    )
+            w_rows[s] = sbuf("w_rows%d" % s, [P, D], BF16)
+            nc.scalar.copy(out=w_rows[s][:].bitcast(F32), in_=t[:])
+
+        def copy_turned(s, tile):
+            t = sbuf("moved_%d_%d" % (s, tile), [P, D], BF16)
+            nc.scalar.copy(
+                out=t[:].bitcast(F32).rearrange("p (g b u) -> p g b u", g=PASSES, u=2),
+                in_=turned[s, tile][:].rearrange("p (g u b) -> p g b u", g=PASSES, u=2),
+            )
+            if s == 0:
+                raw[tile] = t
+            else:
+                grouped[s, tile] = t
+
+        def weigh_turned(tile):
+            t = sbuf("grouped_0_%d" % tile, [P, D], BF16)
+            src = turned[0, tile][:].bitcast(BF16)
+            for g in range(PASSES):
+                cols = slice(g * CHUNK, (g + 1) * CHUNK)
+                nc.vector.tensor_tensor(
+                    out=t[:, cols].rearrange("p (b u e) -> p b u e", u=2, e=2),
+                    in0=src[:, cols].rearrange("p (u b e) -> p b u e", u=2, e=2),
+                    in1=w_cols[0][:, g, 0:4]
+                    .rearrange("p (u e) -> p u e", u=2)
+                    .unsqueeze(1)
+                    .to_broadcast([P, P, 2, 2]),
+                    op=MULT,
+                )
+            grouped[0, tile] = t
+
+        def weigh_raw(tile):
+            t = sbuf("grouped_0_%d" % tile, [P, D], BF16)
+            nc.vector.tensor_tensor(
+                out=t[:].rearrange("p (g b t) -> p g b t", g=PASSES, t=4),
+                in0=raw[tile][:].rearrange("p (g b t) -> p g b t", g=PASSES, t=4),
+                in1=w_cols[0][:, :, 0:4].unsqueeze(2).to_broadcast([P, PASSES, P, 4]),
+                op=MULT,
+            )
+            grouped[0, tile] = t
+
+        def quantize(s, tile):
+            a_codes[s, tile] = sbuf("a_codes_%d_%d" % (s, tile), [P, PASSES * P], U32)
+            a_scales[s, tile] = sbuf("a_scales_%d_%d" % (s, tile), [P, PASSES * P], U8)
+            nc.vector.quantize_mx(
+                out=a_codes[s, tile][:].bitcast(FP8X4), scales=a_scales[s, tile][:], in_=grouped[s, tile][:]
+            )
+
+        units = [(s, 2 * pair + k) for pair in range(TILES // 2) for s in range(STAGES) for k in range(2)]
+
+        turn(0, 0, (0, 0))
+        weigh_turned(0)
+        quantize(0, 0)
+
+        for n, (s, tile) in enumerate(units):
+            nxt = units[n + 1] if n + 1 < len(units) else None
+            chained = nxt is not None and nxt[0] > 0
+            if s == 0:
+                first, second = (1, True, True), (2, True, True)
+                third, fourth = (3, True, False), (0, True, False)
+            elif s == 1:
+                first, second = (3, False, True), (2, True, True)
+                third, fourth = (0, False, False), (1, True, False)
+            else:
+                first, second = (0, False, True), (1, False, True)
+                third, fourth = (2, True, True), (3, True, True)
+            ahead = tile + 2 if s == STAGES - 1 and tile + 2 < TILES else None
+
+            if ahead is not None:
+                weigh_raw(ahead)
+            mx(s, tile, *first)
+            add_base(s, tile, first[0])
+            if ahead is not None:
+                quantize(0, ahead)
+            mx(s, tile, *second)
+            add_base(s, tile, second[0])
+
+            if n == 0:
+                spread_w(1, (1, 3))
+                turn(0, 1, (1, 0))
+                spread_w(2, (1, 2))
+                weigh_turned(1)
+            if chained:
+                turn(nxt[0], nxt[1], (nxt[1], nxt[0]))
+                copy_turned(*nxt)
+                if nxt[0] == STAGES - 1 and nxt[1] + 2 < TILES:
+                    turn(0, nxt[1] + 2, (nxt[1], 3))
+                    copy_turned(0, nxt[1] + 2)
+
+            mx(s, tile, *third)
+            mx(s, tile, *fourth)
+            if s < STAGES - 1:
+                weigh(s + 1, tile, 0 if s == 0 else 1)
+            if chained or n == 0:
+                quantize(*nxt)
+            if s < STAGES - 1:
+                weigh(s + 1, tile, 1 if s == 0 else 0)
+            else:
+                add_base(s, tile, third[0])
+                add_base(s, tile, fourth[0])

@@ -41,9 +41,17 @@ def tile_schwarz_three_sweep_t2_kernel(
         def sbuf(name, shape, dtype):
             return sb.tile(shape, dtype, name=name, align_bytes=64)
 
-        def bank(tile, chunk):
-            name = "bank_%d_%d" % (tile % 2, chunk)
+        free_banks = list(range(8))
+        held = {}
+
+        def take_bank(user):
+            held[user] = free_banks[0]
+            free_banks.remove(held[user])
+            name = "bank%d" % held[user]
             return psum.tile([P, CHUNK], F32, name=name, tag=name)
+
+        def give_bank(user):
+            free_banks.append(held[user])
 
         ident = sbuf("ident", [P, P], F32)
         make_identity(nc, ident[:])
@@ -85,26 +93,26 @@ def tile_schwarz_three_sweep_t2_kernel(
                 c_codes[s, first + c] = (t, c)
 
         load_r(0, 0)
+        load_r(1, 0)
         load_w(0)
+        load_w(1)
         load_scales(0)
         load_codes(0, 1, 1)
         load_codes(0, 2, 1)
         load_r(0, 1)
-        load_w(1)
-        load_r(1, 0)
-        load_w(2)
         load_codes(0, 3, 1)
-        load_codes(0, 0, 1)
+        load_r(2, 0)
         load_r(1, 1)
+        load_codes(0, 0, 1)
+        load_w(2)
+        load_r(2, 1)
         load_scales(1)
         load_codes(1, 2, 2)
         load_codes(1, 0, 2)
-        load_r(2, 0)
+        load_r(3, 0)
         load_scales(2)
         load_codes(2, 0, 2)
         load_codes(2, 2, 2)
-        load_r(3, 0)
-        load_r(2, 1)
         load_r(3, 1)
 
         base = {}
@@ -115,7 +123,6 @@ def tile_schwarz_three_sweep_t2_kernel(
         w_rows = {}
         sorted_a = {}
         grouped = {}
-        raw = {}
         a_codes = {}
         a_scales = {}
         groups = {}
@@ -123,7 +130,7 @@ def tile_schwarz_three_sweep_t2_kernel(
 
         def mx(s, tile, chunk, start, stop):
             if start:
-                groups[tile, chunk] = bank(tile, chunk)
+                groups[tile, chunk] = take_bank((tile, chunk))
             acc = groups[tile, chunk]
             t, c = c_codes[s, chunk]
             for g in range(PASSES):
@@ -137,14 +144,19 @@ def tile_schwarz_three_sweep_t2_kernel(
                     stop=(stop and g == PASSES - 1),
                 )
 
-        def add_base(s, tile, chunk):
-            t = sbuf("res_%d_%d_%d" % (s, tile, chunk), [P, CHUNK], F32)
-            nc.vector.tensor_tensor(out=t[:], in0=groups[tile, chunk][:], in1=base[tile, chunk], op=ADD)
-            base[tile, chunk] = t[:]
-            if s == STAGES - 1:
-                nc.sync.dma_start(
-                    out=out[tile * P : (tile + 1) * P, chunk * CHUNK : (chunk + 1) * CHUNK], in_=t[:]
+        def add_base(s, tile, chunk, parts=1):
+            width = CHUNK // parts
+            for part in range(parts):
+                cols = slice(part * width, (part + 1) * width)
+                t = sbuf("res_%d_%d_%d_%d" % (s, tile, chunk, part), [P, width], F32)
+                nc.vector.tensor_tensor(
+                    out=t[:], in0=groups[tile, chunk][:, cols], in1=base[tile, chunk][:, cols], op=ADD
                 )
+                if s == STAGES - 1:
+                    first = chunk * CHUNK + part * width
+                    nc.sync.dma_start(out=out[tile * P : (tile + 1) * P, first : first + width], in_=t[:])
+            give_bank((tile, chunk))
+            base[tile, chunk] = t[:]
 
         def weigh(s, tile, g):
             if (s, tile) not in sorted_a:
@@ -157,8 +169,8 @@ def tile_schwarz_three_sweep_t2_kernel(
                 op=MULT,
             )
 
-        def turn(s, tile, at):
-            t = bank(*at)
+        def turn(s, tile):
+            t = take_bank(("turn", s, tile))
             for g in range(PASSES):
                 for u in range(2):
                     j = 2 * g + u
@@ -169,8 +181,8 @@ def tile_schwarz_three_sweep_t2_kernel(
                     nc.tensor.transpose(t[:, j * P : (j + 1) * P], src, ident[:])
             turned[s, tile] = t
 
-        def spread_w(s, at):
-            t = bank(*at)
+        def spread_w(s):
+            t = take_bank(("w", s))
             words = w_cols[s][:].bitcast(F32)
             for g in range(PASSES):
                 for u in range(2):
@@ -180,6 +192,7 @@ def tile_schwarz_three_sweep_t2_kernel(
                     )
             w_rows[s] = sbuf("w_rows%d" % s, [P, D], BF16)
             nc.scalar.copy(out=w_rows[s][:].bitcast(F32), in_=t[:])
+            give_bank(("w", s))
 
         def copy_turned(s, tile):
             t = sbuf("moved_%d_%d" % (s, tile), [P, D], BF16)
@@ -187,10 +200,8 @@ def tile_schwarz_three_sweep_t2_kernel(
                 out=t[:].bitcast(F32).rearrange("p (g b u) -> p g b u", g=PASSES, u=2),
                 in_=turned[s, tile][:].rearrange("p (g u b) -> p g b u", g=PASSES, u=2),
             )
-            if s == 0:
-                raw[tile] = t
-            else:
-                grouped[s, tile] = t
+            give_bank(("turn", s, tile))
+            grouped[s, tile] = t
 
         def weigh_turned(tile):
             t = sbuf("grouped_0_%d" % tile, [P, D], BF16)
@@ -206,16 +217,7 @@ def tile_schwarz_three_sweep_t2_kernel(
                     .to_broadcast([P, P, 2, 2]),
                     op=MULT,
                 )
-            grouped[0, tile] = t
-
-        def weigh_raw(tile):
-            t = sbuf("grouped_0_%d" % tile, [P, D], BF16)
-            nc.vector.tensor_tensor(
-                out=t[:].rearrange("p (g b t) -> p g b t", g=PASSES, t=4),
-                in0=raw[tile][:].rearrange("p (g b t) -> p g b t", g=PASSES, t=4),
-                in1=w_cols[0][:, :, 0:4].unsqueeze(2).to_broadcast([P, PASSES, P, 4]),
-                op=MULT,
-            )
+            give_bank(("turn", 0, tile))
             grouped[0, tile] = t
 
         def quantize(s, tile):
@@ -225,55 +227,58 @@ def tile_schwarz_three_sweep_t2_kernel(
                 out=a_codes[s, tile][:].bitcast(FP8X4), scales=a_scales[s, tile][:], in_=grouped[s, tile][:]
             )
 
-        units = [(s, 2 * pair + k) for pair in range(TILES // 2) for s in range(STAGES) for k in range(2)]
+        units = [(s, d - 2 * s) for d in range(TILES + 2 * STAGES - 2) for s in range(STAGES) if 0 <= d - 2 * s < TILES]
 
-        turn(0, 0, (0, 0))
-        weigh_turned(0)
+        def prepare(s, tile):
+            turn(s, tile)
+            if s == 0:
+                weigh_turned(tile)
+            else:
+                copy_turned(s, tile)
+
+        prepare(0, 0)
         quantize(0, 0)
+        prepare(0, 1)
+        spread_w(1)
+        quantize(0, 1)
+        prepared = 2
 
         for n, (s, tile) in enumerate(units):
-            nxt = units[n + 1] if n + 1 < len(units) else None
-            chained = nxt is not None and nxt[0] > 0
+            fresh = []
+            if prepared == n + 1 and prepared < len(units):
+                fresh = units[prepared : prepared + 1]
+                prepared = prepared + len(fresh)
+            for unit in fresh:
+                prepare(*unit)
+            if n == 3:
+                spread_w(2)
+            closing = ((1, 2), (3, 2), (1, 2))[s]
+            mx(s, tile, closing[0], s == 0, True)
+            add_base(s, tile, closing[0])
+            mx(s, tile, closing[1], True, True)
+            if 0 < n < len(units) - 1:
+                quantize(*units[n + 1])
+            add_base(s, tile, closing[1])
             if s == 0:
-                first, second = (1, True, True), (2, True, True)
-                third, fourth = (3, True, False), (0, True, False)
+                mx(0, tile, 3, True, False)
+                if n == 1:
+                    for early in range(2):
+                        mx(0, early, 0, True, False)
             elif s == 1:
-                first, second = (3, False, True), (2, True, True)
-                third, fourth = (0, False, False), (1, True, False)
+                if 2 <= tile < 2:
+                    mx(0, tile, 0, True, False)
+                if tile < 2:
+                    mx(1, tile, 0, False, False)
+                mx(1, tile, 1, True, False)
             else:
-                first, second = (0, False, True), (1, False, True)
-                third, fourth = (2, True, True), (3, True, True)
-            ahead = tile + 2 if s == STAGES - 1 and tile + 2 < TILES else None
-
-            if ahead is not None:
-                weigh_raw(ahead)
-            mx(s, tile, *first)
-            add_base(s, tile, first[0])
-            if ahead is not None:
-                quantize(0, ahead)
-            mx(s, tile, *second)
-            add_base(s, tile, second[0])
-
-            if n == 0:
-                spread_w(1, (1, 3))
-                turn(0, 1, (1, 0))
-                spread_w(2, (1, 2))
-                weigh_turned(1)
-            if chained:
-                turn(nxt[0], nxt[1], (nxt[1], nxt[0]))
-                copy_turned(*nxt)
-                if nxt[0] == STAGES - 1 and nxt[1] + 2 < TILES:
-                    turn(0, nxt[1] + 2, (nxt[1], 3))
-                    copy_turned(0, nxt[1] + 2)
-
-            mx(s, tile, *third)
-            mx(s, tile, *fourth)
+                mx(2, tile, 3, True, True)
+                if tile >= 2:
+                    mx(0, tile, 0, True, False)
+                    mx(1, tile, 0, False, False)
+                mx(2, tile, 0, False, True)
             if s < STAGES - 1:
-                weigh(s + 1, tile, 0 if s == 0 else 1)
-            if chained or n == 0:
-                quantize(*nxt)
-            if s < STAGES - 1:
-                weigh(s + 1, tile, 1 if s == 0 else 0)
+                weigh(s + 1, tile, s)
+                weigh(s + 1, tile, 1 - s)
             else:
-                add_base(s, tile, third[0])
-                add_base(s, tile, fourth[0])
+                add_base(s, tile, 3)
+                add_base(s, tile, 0, 2 if n == len(units) - 1 else 1)

@@ -3,7 +3,7 @@ from contextlib import ExitStack
 import concourse.mybir as mybir
 from concourse.masks import make_identity
 
-B, N, D, H = 512, 2048, 1024, 512
+B, N, D = 512, 2048, 1024
 FLOPS = 3 * 2 * B * D * N
 
 F32 = mybir.dt.float32
@@ -17,12 +17,18 @@ ADD = mybir.AluOpType.add
 MULT = mybir.AluOpType.mult
 
 P = 128
+PACK = 4
 CHUNK = 512
 CHUNKS = N // CHUNK
 PASSES = D // CHUNK
 TILES = B // P
 STAGES = 3
+BANKS = 8
+CODE_BYTES = 2 * CHUNK
 W_ROW = 16
+STAGE_LAG = 2
+EARLY_TILES = 2
+LAST_PARTS = 2
 
 
 def tile_schwarz_three_sweep_t2_kernel(
@@ -41,56 +47,62 @@ def tile_schwarz_three_sweep_t2_kernel(
         def sbuf(name, shape, dtype):
             return sb.tile(shape, dtype, name=name, align_bytes=64)
 
-        free_banks = list(range(8))
-        held = {}
+        free_banks = list(range(BANKS))
+        bank_of = {}
 
         def take_bank(user):
-            held[user] = free_banks[0]
-            free_banks.remove(held[user])
-            name = "bank%d" % held[user]
+            bank_of[user] = free_banks[0]
+            free_banks.remove(bank_of[user])
+            name = "bank%d" % bank_of[user]
             return psum.tile([P, CHUNK], F32, name=name, tag=name)
 
         def give_bank(user):
-            free_banks.append(held[user])
+            free_banks.append(bank_of[user])
 
         ident = sbuf("ident", [P, P], F32)
         make_identity(nc, ident[:])
 
-        planes = []
+        c_scales = []
         for s in range(STAGES):
-            plane = sbuf("plane%d" % s, [P, PASSES, N], U8)
-            nc.vector.memset(plane[:].bitcast(I32), 0)
-            planes.append(plane)
+            t = sbuf("c_scales%d" % s, [P, PASSES, N], U8)
+            nc.vector.memset(t[:].bitcast(I32), 0)
+            c_scales.append(t)
 
-        r_half = {}
+        residual = {}
+        r_low = {}
         w_cols = {}
         c_codes = {}
 
         def load_r(tile, half):
             t = sbuf("r_%d_%d" % (tile, half), [P, D], BF16)
             nc.sync.dma_start(out=t[:], in_=r[tile * P : (tile + 1) * P, half * D : (half + 1) * D])
-            r_half[tile, half] = t
+            if half == 0:
+                r_low[tile] = t
+            for c in range(PASSES):
+                residual[tile, PASSES * half + c] = t[:, c * CHUNK : (c + 1) * CHUNK]
 
         def load_w(s):
-            t = sbuf("w_cols%d" % s, [P, PASSES, W_ROW], BF16)
-            nc.sync.dma_start(out=t[:, :, 0:4], in_=w_dram[s].rearrange("(g p t) -> p g t", g=PASSES, t=4))
-            w_cols[s] = t
+            w_cols[s] = sbuf("w_cols%d" % s, [P, PASSES, W_ROW], BF16)
+            nc.sync.dma_start(
+                out=w_cols[s][:, :, 0:PACK], in_=w_dram[s].rearrange("(g p t) -> p g t", g=PASSES, t=PACK)
+            )
 
         def load_scales(s):
-            src = scales_dram[s].bitcast(I32).rearrange("g (q r) n -> r q g n", r=4)
-            dst = planes[s][:].bitcast(I32)
-            for row in range(4):
-                nc.sync.dma_start(out=dst[row:P:32, :, :], in_=src[row])
+            src = scales_dram[s].bitcast(I32).rearrange("g (q j) n -> j q g n", j=4)
+            dst = c_scales[s][:].bitcast(I32)
+            for j in range(4):
+                nc.sync.dma_start(out=dst[j:P:32, :, :], in_=src[j])
 
         def load_codes(s, first, count):
-            t = sbuf("codes_%d_%d" % (s, first), [P, PASSES, count * 2 * CHUNK], U8)
+            t = sbuf("c_codes_%d_%d" % (s, first), [P, PASSES, count * CODE_BYTES], U8)
             src = words_dram[s].bitcast(I32).rearrange("g p n -> p g n")
-            per_chunk = 2 * CHUNK // 4
             nc.sync.dma_start(
-                out=t[:].bitcast(I32), in_=src[:, :, first * per_chunk : (first + count) * per_chunk]
+                out=t[:].bitcast(I32),
+                in_=src[:, :, first * CODE_BYTES // 4 : (first + count) * CODE_BYTES // 4],
             )
-            for c in range(count):
-                c_codes[s, first + c] = (t, c)
+            for g in range(PASSES):
+                for c in range(count):
+                    c_codes[s, first + c, g] = t[:, g, c * CODE_BYTES : (c + 1) * CODE_BYTES]
 
         load_r(0, 0)
         load_r(1, 0)
@@ -104,181 +116,166 @@ def tile_schwarz_three_sweep_t2_kernel(
         load_r(2, 0)
         load_r(1, 1)
         load_codes(0, 0, 1)
-        load_w(2)
         load_r(2, 1)
+        load_r(3, 0)
+        load_w(2)
         load_scales(1)
         load_codes(1, 2, 2)
         load_codes(1, 0, 2)
-        load_r(3, 0)
-        load_scales(2)
-        load_codes(2, 0, 2)
-        load_codes(2, 2, 2)
         load_r(3, 1)
-
-        base = {}
-        for tile in range(TILES):
-            for c in range(CHUNKS):
-                base[tile, c] = r_half[tile, c // 2][:, (c % 2) * CHUNK : (c % 2 + 1) * CHUNK]
+        load_scales(2)
+        load_codes(2, 1, 2)
+        load_codes(2, 3, 1)
+        load_codes(2, 0, 1)
 
         w_rows = {}
-        sorted_a = {}
-        grouped = {}
+        weighted = {}
+        k_major = {}
         a_codes = {}
         a_scales = {}
         groups = {}
-        turned = {}
 
-        def mx(s, tile, chunk, start, stop):
+        def multiply(s, tile, chunk, start, stop):
             if start:
                 groups[tile, chunk] = take_bank((tile, chunk))
-            acc = groups[tile, chunk]
-            t, c = c_codes[s, chunk]
             for g in range(PASSES):
+                rows = slice(g * P, (g + 1) * P)
                 nc.tensor.matmul_mx(
-                    out=acc[:],
-                    lhsT=a_codes[s, tile][:, g * P : (g + 1) * P].bitcast(FP8X4),
-                    lhsT_scale=a_scales[s, tile][:, g * P : (g + 1) * P],
-                    rhs=t[:, g, c * 2 * CHUNK : (c + 1) * 2 * CHUNK].bitcast(FP4X4),
-                    rhs_scale=planes[s][:, g, chunk * CHUNK : (chunk + 1) * CHUNK],
+                    out=groups[tile, chunk][:],
+                    lhsT=a_codes[s, tile][:, rows].bitcast(FP8X4),
+                    lhsT_scale=a_scales[s, tile][:, rows],
+                    rhs=c_codes[s, chunk, g].bitcast(FP4X4),
+                    rhs_scale=c_scales[s][:, g, chunk * CHUNK : (chunk + 1) * CHUNK],
                     start=(start and g == 0),
                     stop=(stop and g == PASSES - 1),
                 )
 
-        def add_base(s, tile, chunk, parts=1):
+        def update(s, tile, chunk):
+            t = sbuf("sum_%d_%d_%d" % (s, tile, chunk), [P, CHUNK], F32)
+            nc.vector.tensor_tensor(out=t[:], in0=groups[tile, chunk][:], in1=residual[tile, chunk], op=ADD)
+            give_bank((tile, chunk))
+            residual[tile, chunk] = t[:]
+
+        def finish(tile, chunk, parts):
             width = CHUNK // parts
             for part in range(parts):
                 cols = slice(part * width, (part + 1) * width)
-                t = sbuf("res_%d_%d_%d_%d" % (s, tile, chunk, part), [P, width], F32)
+                t = sbuf("out_%d_%d_%d" % (tile, chunk, part), [P, width], F32)
                 nc.vector.tensor_tensor(
-                    out=t[:], in0=groups[tile, chunk][:, cols], in1=base[tile, chunk][:, cols], op=ADD
+                    out=t[:], in0=groups[tile, chunk][:, cols], in1=residual[tile, chunk][:, cols], op=ADD
                 )
-                if s == STAGES - 1:
-                    first = chunk * CHUNK + part * width
-                    nc.sync.dma_start(out=out[tile * P : (tile + 1) * P, first : first + width], in_=t[:])
+                first = chunk * CHUNK + part * width
+                nc.sync.dma_start(out=out[tile * P : (tile + 1) * P, first : first + width], in_=t[:])
             give_bank((tile, chunk))
-            base[tile, chunk] = t[:]
 
-        def weigh(s, tile, g):
-            if (s, tile) not in sorted_a:
-                sorted_a[s, tile] = sbuf("sorted_%d_%d" % (s, tile), [P, D], BF16)
+        def weigh(engine, s, tile, g, parities):
             cols = slice(g * CHUNK, (g + 1) * CHUNK)
-            nc.vector.tensor_tensor(
-                out=sorted_a[s, tile][:, cols].rearrange("p (u m e) -> p u m e", u=2, e=2),
-                in0=base[tile, s + g].rearrange("p (m u e) -> p u m e", u=2, e=2),
-                in1=w_rows[s][:, cols].rearrange("p (u m e) -> p u m e", u=2, e=2),
+            engine.tensor_tensor(
+                out=weighted[s, tile][:, cols].rearrange("b (u p e) -> b u p e", u=2, e=2)[:, parities],
+                in0=residual[tile, s + g].rearrange("b (p u e) -> b u p e", u=2, e=2)[:, parities],
+                in1=w_rows[s][:, cols].rearrange("b (u p e) -> b u p e", u=2, e=2)[:, parities],
                 op=MULT,
             )
 
-        def turn(s, tile):
-            t = take_bank(("turn", s, tile))
-            for g in range(PASSES):
-                for u in range(2):
-                    j = 2 * g + u
-                    if s == 0:
-                        src = r_half[tile, 0][:].bitcast(F32)[:, 2 * P * g + u : 2 * P * (g + 1) : 2]
-                    else:
-                        src = sorted_a[s, tile][:].bitcast(F32)[:, j * P : (j + 1) * P]
-                    nc.tensor.transpose(t[:, j * P : (j + 1) * P], src, ident[:])
-            turned[s, tile] = t
-
         def spread_w(s):
-            t = take_bank(("w", s))
+            bank = take_bank(("w", s))
             words = w_cols[s][:].bitcast(F32)
             for g in range(PASSES):
                 for u in range(2):
                     j = 2 * g + u
                     nc.tensor.transpose(
-                        t[:, j * P : (j + 1) * P], words[:, g, u : u + 1].to_broadcast([P, P]), ident[:]
+                        bank[:, j * P : (j + 1) * P], words[:, g, u : u + 1].to_broadcast([P, P]), ident[:]
                     )
             w_rows[s] = sbuf("w_rows%d" % s, [P, D], BF16)
-            nc.scalar.copy(out=w_rows[s][:].bitcast(F32), in_=t[:])
+            nc.scalar.copy(out=w_rows[s][:].bitcast(F32), in_=bank[:])
             give_bank(("w", s))
 
-        def copy_turned(s, tile):
-            t = sbuf("moved_%d_%d" % (s, tile), [P, D], BF16)
-            nc.scalar.copy(
-                out=t[:].bitcast(F32).rearrange("p (g b u) -> p g b u", g=PASSES, u=2),
-                in_=turned[s, tile][:].rearrange("p (g u b) -> p g b u", g=PASSES, u=2),
-            )
-            give_bank(("turn", s, tile))
-            grouped[s, tile] = t
-
-        def weigh_turned(tile):
-            t = sbuf("grouped_0_%d" % tile, [P, D], BF16)
-            src = turned[0, tile][:].bitcast(BF16)
+        def turn(s, tile):
+            bank = take_bank(("turn", s, tile))
             for g in range(PASSES):
-                cols = slice(g * CHUNK, (g + 1) * CHUNK)
-                nc.vector.tensor_tensor(
-                    out=t[:, cols].rearrange("p (b u e) -> p b u e", u=2, e=2),
-                    in0=src[:, cols].rearrange("p (u b e) -> p b u e", u=2, e=2),
-                    in1=w_cols[0][:, g, 0:4]
-                    .rearrange("p (u e) -> p u e", u=2)
-                    .unsqueeze(1)
-                    .to_broadcast([P, P, 2, 2]),
-                    op=MULT,
+                for u in range(2):
+                    j = 2 * g + u
+                    if s == 0:
+                        words = r_low[tile][:].bitcast(F32)[:, 2 * P * g + u : 2 * P * (g + 1) : 2]
+                    else:
+                        words = weighted[s, tile][:].bitcast(F32)[:, j * P : (j + 1) * P]
+                    nc.tensor.transpose(bank[:, j * P : (j + 1) * P], words, ident[:])
+            k_major[s, tile] = sbuf("k_major_%d_%d" % (s, tile), [P, D], BF16)
+            if s == 0:
+                for g in range(PASSES):
+                    cols = slice(g * CHUNK, (g + 1) * CHUNK)
+                    w_pairs = w_cols[0][:, g, 0:PACK].rearrange("p (u e) -> p u e", u=2)
+                    nc.vector.tensor_tensor(
+                        out=k_major[0, tile][:, cols].rearrange("p (b u e) -> p b u e", u=2, e=2),
+                        in0=bank[:].bitcast(BF16)[:, cols].rearrange("p (u b e) -> p b u e", u=2, e=2),
+                        in1=w_pairs.unsqueeze(1).to_broadcast([P, P, 2, 2]),
+                        op=MULT,
+                    )
+            else:
+                nc.scalar.copy(
+                    out=k_major[s, tile][:].bitcast(F32).rearrange("p (g b u) -> p g b u", g=PASSES, u=2),
+                    in_=bank[:].rearrange("p (g u b) -> p g b u", g=PASSES, u=2),
                 )
-            give_bank(("turn", 0, tile))
-            grouped[0, tile] = t
+            give_bank(("turn", s, tile))
 
         def quantize(s, tile):
             a_codes[s, tile] = sbuf("a_codes_%d_%d" % (s, tile), [P, PASSES * P], U32)
             a_scales[s, tile] = sbuf("a_scales_%d_%d" % (s, tile), [P, PASSES * P], U8)
             nc.vector.quantize_mx(
-                out=a_codes[s, tile][:].bitcast(FP8X4), scales=a_scales[s, tile][:], in_=grouped[s, tile][:]
+                out=a_codes[s, tile][:].bitcast(FP8X4), scales=a_scales[s, tile][:], in_=k_major[s, tile][:]
             )
 
-        units = [(s, d - 2 * s) for d in range(TILES + 2 * STAGES - 2) for s in range(STAGES) if 0 <= d - 2 * s < TILES]
+        steps = sorted(
+            ((s, tile) for s in range(STAGES) for tile in range(TILES)),
+            key=lambda step: (step[1] + STAGE_LAG * step[0], step[0]),
+        )
 
-        def prepare(s, tile):
-            turn(s, tile)
-            if s == 0:
-                weigh_turned(tile)
-            else:
-                copy_turned(s, tile)
-
-        prepare(0, 0)
-        quantize(0, 0)
-        prepare(0, 1)
+        turn(*steps[0])
+        quantize(*steps[0])
+        turn(*steps[1])
         spread_w(1)
-        quantize(0, 1)
-        prepared = 2
+        quantize(*steps[1])
 
-        for n, (s, tile) in enumerate(units):
-            fresh = []
-            if prepared == n + 1 and prepared < len(units):
-                fresh = units[prepared : prepared + 1]
-                prepared = prepared + len(fresh)
-            for unit in fresh:
-                prepare(*unit)
-            if n == 3:
+        for n, (s, tile) in enumerate(steps):
+            ahead = steps[n + 1 : n + 2] if n > 0 else []
+            for step in ahead:
+                turn(*step)
+            if (s, tile) == (1, 0):
                 spread_w(2)
-            closing = ((1, 2), (3, 2), (1, 2))[s]
-            mx(s, tile, closing[0], s == 0, True)
-            add_base(s, tile, closing[0])
-            mx(s, tile, closing[1], True, True)
-            if 0 < n < len(units) - 1:
-                quantize(*units[n + 1])
-            add_base(s, tile, closing[1])
-            if s == 0:
-                mx(0, tile, 3, True, False)
-                if n == 1:
-                    for early in range(2):
-                        mx(0, early, 0, True, False)
-            elif s == 1:
-                if 2 <= tile < 2:
-                    mx(0, tile, 0, True, False)
-                if tile < 2:
-                    mx(1, tile, 0, False, False)
-                mx(1, tile, 1, True, False)
-            else:
-                mx(2, tile, 3, True, True)
-                if tile >= 2:
-                    mx(0, tile, 0, True, False)
-                    mx(1, tile, 0, False, False)
-                mx(2, tile, 0, False, True)
+
             if s < STAGES - 1:
-                weigh(s + 1, tile, s)
-                weigh(s + 1, tile, 1 - s)
+                first_pass = s
+                first, second = s + 1 + first_pass, s + 2 - first_pass
+                weighted[s + 1, tile] = sbuf("weighted_%d_%d" % (s + 1, tile), [P, D], BF16)
+                multiply(s, tile, first, s == 0, True)
+                update(s, tile, first)
+                multiply(s, tile, second, True, True)
+                for step in ahead:
+                    quantize(*step)
+                update(s, tile, second)
+                weigh(nc.gpsimd, s + 1, tile, first_pass, slice(0, 1))
+                weigh(nc.vector, s + 1, tile, first_pass, slice(1, 2))
+                weigh(nc.gpsimd, s + 1, tile, 1 - first_pass, slice(0, 2))
+                if s == 0:
+                    multiply(0, tile, 3, True, False)
+                    if tile == EARLY_TILES - 1:
+                        for early in range(EARLY_TILES):
+                            multiply(0, early, 0, True, False)
+                else:
+                    if tile < EARLY_TILES:
+                        multiply(1, tile, 0, False, False)
+                    multiply(1, tile, 1, True, False)
             else:
-                add_base(s, tile, 3)
-                add_base(s, tile, 0, 2 if n == len(units) - 1 else 1)
+                multiply(s, tile, 1, False, True)
+                finish(tile, 1, 1)
+                multiply(s, tile, 2, True, True)
+                for step in ahead:
+                    quantize(*step)
+                finish(tile, 2, 1)
+                multiply(s, tile, 3, True, True)
+                if tile >= EARLY_TILES:
+                    multiply(0, tile, 0, True, False)
+                    multiply(1, tile, 0, False, False)
+                multiply(s, tile, 0, False, True)
+                finish(tile, 3, 1)
+                finish(tile, 0, LAST_PARTS if tile == TILES - 1 else 1)

from contextlib import ExitStack

import concourse.mybir as mybir
from concourse.masks import make_identity

B, N, D = 512, 2048, 1024
FLOPS = 3 * 2 * B * D * N

F32 = mybir.dt.float32
BF16 = mybir.dt.bfloat16
I32 = mybir.dt.int32
U32 = mybir.dt.uint32
U8 = mybir.dt.uint8
FP8X4 = mybir.dt.float8_e4m3fn_x4
FP4X4 = mybir.dt.float4_e2m1fn_x4
ADD = mybir.AluOpType.add
MULT = mybir.AluOpType.mult

P = 128
PACK = 4
CHUNK = 512
CHUNKS = N // CHUNK
PASSES = D // CHUNK
TILES = B // P
STAGES = 3
BANKS = 8
CODE_BYTES = 2 * CHUNK
W_ROW = 16
STAGE_LAG = 2
EARLY_TILES = 2
LAST_PARTS = 2


def tile_schwarz_three_sweep_t2_kernel(
    tc, r, w1, w2, w3, c1_words, c1_scales, c2_words, c2_scales, c3_words, c3_scales, out
):
    nc = tc.nc
    w_dram = (w1, w2, w3)
    words_dram = (c1_words, c2_words, c3_words)
    scales_dram = (c1_scales, c2_scales, c3_scales)

    with ExitStack() as ctx:
        sb = ctx.enter_context(tc.tile_pool(name="sb", bufs=1))
        psum = ctx.enter_context(tc.psum_pool(name="psum", bufs=1))
        ctx.enter_context(tc.manual_schedule())

        def sbuf(name, shape, dtype):
            return sb.tile(shape, dtype, name=name, align_bytes=64)

        free_banks = list(range(BANKS))
        bank_of = {}

        def take_bank(user):
            bank_of[user] = free_banks[0]
            free_banks.remove(bank_of[user])
            name = "bank%d" % bank_of[user]
            return psum.tile([P, CHUNK], F32, name=name, tag=name)

        def give_bank(user):
            free_banks.append(bank_of[user])

        ident = sbuf("ident", [P, P], F32)
        make_identity(nc, ident[:])

        c_scales = []
        for s in range(STAGES):
            t = sbuf("c_scales%d" % s, [P, PASSES, N], U8)
            nc.vector.memset(t[:].bitcast(I32), 0)
            c_scales.append(t)

        residual = {}
        r_low = {}
        w_cols = {}
        c_codes = {}

        def load_r(tile, half):
            t = sbuf("r_%d_%d" % (tile, half), [P, D], BF16)
            nc.sync.dma_start(out=t[:], in_=r[tile * P : (tile + 1) * P, half * D : (half + 1) * D])
            if half == 0:
                r_low[tile] = t
            for c in range(PASSES):
                residual[tile, PASSES * half + c] = t[:, c * CHUNK : (c + 1) * CHUNK]

        def load_w(s):
            w_cols[s] = sbuf("w_cols%d" % s, [P, PASSES, W_ROW], BF16)
            nc.sync.dma_start(
                out=w_cols[s][:, :, 0:PACK], in_=w_dram[s].rearrange("(g p t) -> p g t", g=PASSES, t=PACK)
            )

        def load_scales(s):
            src = scales_dram[s].bitcast(I32).rearrange("g (q j) n -> j q g n", j=4)
            dst = c_scales[s][:].bitcast(I32)
            for j in range(4):
                nc.sync.dma_start(out=dst[j:P:32, :, :], in_=src[j])

        def load_codes(s, first, count):
            t = sbuf("c_codes_%d_%d" % (s, first), [P, PASSES, count * CODE_BYTES], U8)
            src = words_dram[s].bitcast(I32).rearrange("g p n -> p g n")
            nc.sync.dma_start(
                out=t[:].bitcast(I32),
                in_=src[:, :, first * CODE_BYTES // 4 : (first + count) * CODE_BYTES // 4],
            )
            for g in range(PASSES):
                for c in range(count):
                    c_codes[s, first + c, g] = t[:, g, c * CODE_BYTES : (c + 1) * CODE_BYTES]

        load_r(0, 0)
        load_r(1, 0)
        load_w(0)
        load_w(1)
        load_scales(0)
        load_codes(0, 1, 1)
        load_codes(0, 2, 1)
        load_r(0, 1)
        load_codes(0, 3, 1)
        load_r(2, 0)
        load_r(1, 1)
        load_codes(0, 0, 1)
        load_r(2, 1)
        load_r(3, 0)
        load_w(2)
        load_scales(1)
        load_codes(1, 2, 2)
        load_codes(1, 0, 2)
        load_r(3, 1)
        load_scales(2)
        load_codes(2, 1, 2)
        load_codes(2, 3, 1)
        load_codes(2, 0, 1)

        w_rows = {}
        weighted = {}
        k_major = {}
        a_codes = {}
        a_scales = {}
        groups = {}

        def multiply(s, tile, chunk, start, stop):
            if start:
                groups[tile, chunk] = take_bank((tile, chunk))
            for g in range(PASSES):
                rows = slice(g * P, (g + 1) * P)
                nc.tensor.matmul_mx(
                    out=groups[tile, chunk][:],
                    lhsT=a_codes[s, tile][:, rows].bitcast(FP8X4),
                    lhsT_scale=a_scales[s, tile][:, rows],
                    rhs=c_codes[s, chunk, g].bitcast(FP4X4),
                    rhs_scale=c_scales[s][:, g, chunk * CHUNK : (chunk + 1) * CHUNK],
                    start=(start and g == 0),
                    stop=(stop and g == PASSES - 1),
                )

        def update(s, tile, chunk):
            t = sbuf("sum_%d_%d_%d" % (s, tile, chunk), [P, CHUNK], F32)
            nc.vector.tensor_tensor(out=t[:], in0=groups[tile, chunk][:], in1=residual[tile, chunk], op=ADD)
            give_bank((tile, chunk))
            residual[tile, chunk] = t[:]

        def finish(tile, chunk, parts):
            width = CHUNK // parts
            for part in range(parts):
                cols = slice(part * width, (part + 1) * width)
                t = sbuf("out_%d_%d_%d" % (tile, chunk, part), [P, width], F32)
                nc.vector.tensor_tensor(
                    out=t[:], in0=groups[tile, chunk][:, cols], in1=residual[tile, chunk][:, cols], op=ADD
                )
                first = chunk * CHUNK + part * width
                nc.sync.dma_start(out=out[tile * P : (tile + 1) * P, first : first + width], in_=t[:])
            give_bank((tile, chunk))

        def weigh(engine, s, tile, g, parities):
            cols = slice(g * CHUNK, (g + 1) * CHUNK)
            engine.tensor_tensor(
                out=weighted[s, tile][:, cols].rearrange("b (u p e) -> b u p e", u=2, e=2)[:, parities],
                in0=residual[tile, s + g].rearrange("b (p u e) -> b u p e", u=2, e=2)[:, parities],
                in1=w_rows[s][:, cols].rearrange("b (u p e) -> b u p e", u=2, e=2)[:, parities],
                op=MULT,
            )

        def spread_w(s):
            bank = take_bank(("w", s))
            words = w_cols[s][:].bitcast(F32)
            for g in range(PASSES):
                for u in range(2):
                    j = 2 * g + u
                    nc.tensor.transpose(
                        bank[:, j * P : (j + 1) * P], words[:, g, u : u + 1].to_broadcast([P, P]), ident[:]
                    )
            w_rows[s] = sbuf("w_rows%d" % s, [P, D], BF16)
            nc.scalar.copy(out=w_rows[s][:].bitcast(F32), in_=bank[:])
            give_bank(("w", s))

        def turn(s, tile):
            bank = take_bank(("turn", s, tile))
            for g in range(PASSES):
                for u in range(2):
                    j = 2 * g + u
                    if s == 0:
                        words = r_low[tile][:].bitcast(F32)[:, 2 * P * g + u : 2 * P * (g + 1) : 2]
                    else:
                        words = weighted[s, tile][:].bitcast(F32)[:, j * P : (j + 1) * P]
                    nc.tensor.transpose(bank[:, j * P : (j + 1) * P], words, ident[:])
            k_major[s, tile] = sbuf("k_major_%d_%d" % (s, tile), [P, D], BF16)
            if s == 0:
                for g in range(PASSES):
                    cols = slice(g * CHUNK, (g + 1) * CHUNK)
                    w_pairs = w_cols[0][:, g, 0:PACK].rearrange("p (u e) -> p u e", u=2)
                    nc.vector.tensor_tensor(
                        out=k_major[0, tile][:, cols].rearrange("p (b u e) -> p b u e", u=2, e=2),
                        in0=bank[:].bitcast(BF16)[:, cols].rearrange("p (u b e) -> p b u e", u=2, e=2),
                        in1=w_pairs.unsqueeze(1).to_broadcast([P, P, 2, 2]),
                        op=MULT,
                    )
            else:
                nc.scalar.copy(
                    out=k_major[s, tile][:].bitcast(F32).rearrange("p (g b u) -> p g b u", g=PASSES, u=2),
                    in_=bank[:].rearrange("p (g u b) -> p g b u", g=PASSES, u=2),
                )
            give_bank(("turn", s, tile))

        def quantize(s, tile):
            a_codes[s, tile] = sbuf("a_codes_%d_%d" % (s, tile), [P, PASSES * P], U32)
            a_scales[s, tile] = sbuf("a_scales_%d_%d" % (s, tile), [P, PASSES * P], U8)
            nc.vector.quantize_mx(
                out=a_codes[s, tile][:].bitcast(FP8X4), scales=a_scales[s, tile][:], in_=k_major[s, tile][:]
            )

        steps = sorted(
            ((s, tile) for s in range(STAGES) for tile in range(TILES)),
            key=lambda step: (step[1] + STAGE_LAG * step[0], step[0]),
        )

        turn(*steps[0])
        quantize(*steps[0])
        turn(*steps[1])
        spread_w(1)
        quantize(*steps[1])

        for n, (s, tile) in enumerate(steps):
            ahead = steps[n + 1 : n + 2] if n > 0 else []
            for step in ahead:
                turn(*step)
            if (s, tile) == (1, 0):
                spread_w(2)

            if s < STAGES - 1:
                first_pass = s
                first, second = s + 1 + first_pass, s + 2 - first_pass
                weighted[s + 1, tile] = sbuf("weighted_%d_%d" % (s + 1, tile), [P, D], BF16)
                multiply(s, tile, first, s == 0, True)
                update(s, tile, first)
                multiply(s, tile, second, True, True)
                for step in ahead:
                    quantize(*step)
                update(s, tile, second)
                weigh(nc.gpsimd, s + 1, tile, first_pass, slice(0, 1))
                weigh(nc.vector, s + 1, tile, first_pass, slice(1, 2))
                weigh(nc.gpsimd, s + 1, tile, 1 - first_pass, slice(0, 2))
                if s == 0:
                    multiply(0, tile, 3, True, False)
                    if tile == EARLY_TILES - 1:
                        for early in range(EARLY_TILES):
                            multiply(0, early, 0, True, False)
                else:
                    if tile < EARLY_TILES:
                        multiply(1, tile, 0, False, False)
                    multiply(1, tile, 1, True, False)
            else:
                multiply(s, tile, 1, False, True)
                finish(tile, 1, 1)
                multiply(s, tile, 2, True, True)
                for step in ahead:
                    quantize(*step)
                finish(tile, 2, 1)
                multiply(s, tile, 3, True, True)
                if tile >= EARLY_TILES:
                    multiply(0, tile, 0, True, False)
                    multiply(1, tile, 0, False, False)
                multiply(s, tile, 0, False, True)
                finish(tile, 3, 1)
                finish(tile, 0, LAST_PARTS if tile == TILES - 1 else 1)
